import numpy as np, ml_dtypes
CORES = [33,38,57,62,81,86,161,166,185,190,209,214]
N = 12
import mx_ref
BF = ml_dtypes.bfloat16
def entries(a):
    return np.ascontiguousarray(a.T).reshape(-1)
def table(e):
    return np.ascontiguousarray(np.reshape(e, (-1, 16)).T).astype(np.int32)
def cols(t, e):
    v = np.concatenate([t.reshape(128, -1, 4), np.zeros((128, 1, 4), BF)], axis=1)
    return np.ascontiguousarray(v[:, e]).reshape(128, -1)
def f(rng, *shape):
    return mx_ref.flush((rng.standard_normal(shape, dtype=np.float32) * np.exp2(rng.integers(-2, 3, shape[:-1] + (1,)))).astype(BF))
def wide(rng, *shape, cols=0):
    v = rng.standard_normal(shape, dtype=np.float32) * np.exp2(rng.integers(-12, 13, shape)).astype(np.float32)
    if cols: v *= np.repeat(np.exp2(rng.integers(-cols, cols + 1, shape[:-2] + (1, shape[-1] // 4))) * (rng.random(shape[:-2] + (1, shape[-1] // 4)) > 0.0625), 4, axis=-1).astype(np.float32)
    return mx_ref.flush(v.astype(BF))
T, W, UN, CR = 512, 512, 160, 64
HOST = [0 if k < 128 else 1 for k in CORES]
def lists(rng, full=False, alike=False):
    uni, need, pos = np.full((N, 2, UN), -1), np.full((N, N, CR), -1), []
    for q in range(N):
        for g in range(2):
            mates = [r for r in range(N) if HOST[r] == g]
            n = UN if full else int(rng.integers(CR >> 1, CR + 1)) if alike else int(rng.integers(UN >> 2, UN + 1))
            at = rng.permutation(UN)[:n]
            uni[q, g, at] = rng.permutation(T)[:n]
            who = rng.permutation(np.repeat(np.arange(len(mates)), CR))[:n]
            for i, r in enumerate(mates):
                e, others = at[who == i], at[who != i]
                if alike: e = at
                else:
                    k = CR if full else int(rng.integers(max(len(e), CR >> 2), min(CR, n) + 1))
                    e = np.concatenate([e, rng.permutation(others)[:k - len(e)]])
                need[r, q, rng.permutation(CR)[:len(e)]] = e
    for r in range(N):
        ok = np.flatnonzero(need[r].reshape(-1) >= 0)
        pos.append(table(rng.permutation(ok)[:W] if full else rng.choice(ok, W)))
    return {"uni": np.stack([table(e.reshape(-1)) for e in uni]), "need": np.stack([table(e.reshape(-1)) for e in need]), "pos": np.stack(pos)}
def setup_inputs(rng):
    return {"c": f(rng, N, 128, 4 * T), "w": f(rng, N, 128, 512), **lists(rng)}
def setup_inputs_alike(rng):
    return {**setup_inputs(rng), **lists(rng, alike=True)}
def setup_inputs_pairs(rng):
    d = setup_inputs(rng)
    uni, need = np.full((N, 2, UN), -1), np.full((N, N, CR), -1)
    for g in range(2):
        mates = rng.permutation([r for r in range(N) if HOST[r] == g])
        for q in range(N):
            at = rng.permutation(UN)[:2 * CR]
            uni[q, g, at] = rng.permutation(T)[:2 * CR]
            for i, r in enumerate(mates):
                need[r, q] = rng.permutation(at[:CR] if i < len(mates) // 2 else at[CR:])
    pos = [table(rng.choice(N * CR, W)) for r in range(N)]
    return {**d, "uni": np.stack([table(e.reshape(-1)) for e in uni]), "need": np.stack([table(e.reshape(-1)) for e in need]), "pos": np.stack(pos)}
def setup_inputs_full(rng):
    return {**setup_inputs(rng), **lists(rng, full=True)}
def setup_inputs_few(rng):
    d = {**setup_inputs(rng), **lists(rng, full=True)}
    uni = np.stack([entries(e) for e in d["uni"]]).reshape(N, 2, UN)
    need = np.stack([entries(e) for e in d["need"]]).reshape(N, N, CR)
    pos = [None] * N
    for g in range(2):
        p = rng.permutation(N)
        h = [HOST[q] for q in p]
        lead = [h.index(0), h.index(1)]
        own = np.concatenate([p[lead], np.delete(p, lead)])[:-(-W // CR)]
        rest = np.setdiff1d(np.arange(N), own)
        uni[rest, g] = -1
        for r in range(N):
            if HOST[r] != g: continue
            need[r, rest] = -1
            s = rng.permutation(own)[:, None] * CR + np.arange(CR)
            s[-1] = rng.permutation(s[-1])
            pos[r] = table(rng.permutation(s.reshape(-1)[:W]))
    return {**d, "uni": np.stack([table(e.reshape(-1)) for e in uni]), "need": np.stack([table(e.reshape(-1)) for e in need]), "pos": np.stack(pos)}
def setup_inputs_spread(rng):
    d = setup_inputs(rng); d["c"] = wide(rng, N, 128, 4 * T, cols=6); return d
def check_inputs(d):
    b = []
    uni = np.stack([entries(e) for e in d["uni"]]).reshape(N, 2, UN)
    need = np.stack([entries(e) for e in d["need"]]).reshape(N, N, CR)
    if uni.min() < -1 or uni.max() >= T: b.append("uni")
    if need.min() < -1 or need.max() >= UN: return b + ["need"]
    for q in range(N):
        for g in range(2):
            e = uni[q, g][uni[q, g] >= 0]
            if len(set(e.tolist())) != len(e): b.append("a column of one owner twice for one host")
            named = set()
            for r in range(N):
                if HOST[r] != g: continue
                k = need[r, q][need[r, q] >= 0]
                if len(set(k.tolist())) != len(k): b.append("need names an entry of one union twice")
                if (uni[q, g][k] < 0).any(): b.append("need names an empty entry of uni")
                named |= set(k.tolist())
            if set(np.flatnonzero(uni[q, g] >= 0).tolist()) - named: b.append("an entry of uni that no rank of the host needs")
    for r in range(N):
        p = entries(d["pos"][r])
        if p.min() < 0 or p.max() >= N * CR or (need[r].reshape(-1)[p] < 0).any(): b.append("pos")
    return b
def reference(c, w, uni, need, pos):
    uni = np.stack([entries(e) for e in uni]).reshape(N, 2, UN)
    need = np.stack([entries(e) for e in need]).reshape(N, N, CR)
    y = np.zeros((N, 128, W), np.float32)
    for r in range(N):
        g = HOST[r]
        t = np.concatenate([cols(c[q], np.where(need[r, q] >= 0, uni[q, g][need[r, q]], -1)) for q in range(N)], axis=1)
        y[r] = mx_ref.matmul(mx_ref.quantize(w[r]), mx_ref.quantize(cols(t, entries(pos[r]))))
    return {"y": y}

from concourse.bass import DstId, RemoteDMATransfer
from concourse.mybir import dt, AluOpType, ActivationFunctionType

UN, CR, W, CT = 160, 64, 512, 512
BK = 2 * CR
COPY = ActivationFunctionType.Copy
CODE, PLANE = "float8_e4m3fn_x4", "uint8"
SCRATCH = {
    "cin": ("sbuf", [128, 4 * CT], "bfloat16"), "win": ("sbuf", [128, 512], "bfloat16"),
    "qc": ("sbuf", [128, CT], CODE), "sc": ("sbuf", [128, CT], PLANE),
    "qw": ("sbuf", [128, 128], CODE), "sw": ("sbuf", [128, 128], PLANE),
    "nd": ("sbuf", [128, 12, 4], "int32"), "lsx": ("sbuf", [128, 6, 8], "uint16"),
    "uni32": ("sbuf", [128, 20], "int32"), "uni16": ("sbuf", [128, 20], "uint16"),
    "pos32": ("sbuf", [128, 32], "int32"), "pt": ("sbuf", [128, 32], "int32"), "pu": ("sbuf", [128, 32], "int32"),
    "pv": ("sbuf", [128, 32], "int32"), "pw": ("sbuf", [128, 32], "int32"), "pos16": ("sbuf", [128, 32], "uint16"),
    "uo": ("sbuf", [128, UN], CODE), "uos": ("sbuf", [128, UN], PLANE),
    "uw": ("sbuf", [128, 2 * UN], CODE), "uws": ("sbuf", [128, 2 * UN], PLANE),
    "ll": ("sbuf", [128, 40], "uint16"),
    "rli": ("sbuf", [128, 6, 8], "uint16"), "rlw": ("sbuf", [128, 8], "uint16"),
    "sd": ("sbuf", [128, 5 * BK], CODE), "sds": ("sbuf", [128, 5 * BK], PLANE),
    "rl": ("sbuf", [128, 2 * BK], CODE), "rls": ("sbuf", [128, 2 * BK], PLANE),
    "land": ("sbuf", [128, 6 * BK], CODE), "lands": ("sbuf", [128, 6 * BK], PLANE),
    "ys": ("sbuf", [128, 6 * BK], "float32"), "yo": ("sbuf", [128, W], "float32"),
    "acc": ("psum", [128, 512 * 6], "float32"),
}
SEMAPHORES = (["ldn", "ldu", "ldp", "ldw", "ldc0", "ldc1", "vnd", "vun", "vps", "vq", "vw", "vuo", "suo", "vuh", "suh",
               "vown", "sown", "auc", "aus", "evv", "evs", "gv", "gs", "st0", "sent", "rlwa", "rlc", "rlp"]
              + ["al%d" % i for i in range(3)] + ["vsd%d" % i for i in range(3)] + ["ssd%d" % i for i in range(3)]
              + ["ap%d" % i for i in range(6)] + ["tm%d" % i for i in range(6)])


def layout(T, topo):
    pairs = []
    for c in T.cores:
        if not pairs or c not in topo.cores_of(pairs[-1][0]):
            pairs.append([])
        pairs[-1].append(c)
    byhost = {}
    for p, m in enumerate(pairs):
        byhost.setdefault(topo.host(m[0]), []).append(p)
    hub = []
    for m in pairs:
        mine = [d for d in T.cores if topo.host(d) == topo.host(m[0])]
        hub.append([c for c in m if all(d == c or topo.may_write(c, d) for d in mine)][0])
    return pairs, byhost, hub


def rank_program(g, core, T, topo):
    pairs, byhost, hub = layout(T, topo)
    sem = T.sem
    here = byhost.get(topo.host(core), [])
    local = [c for p in here for c in pairs[p]]

    def pair_of(c):
        return [p for p, m in enumerate(pairs) if c in m][0]

    def mate_of(c):
        return [d for d in pairs[pair_of(c)] if d != c][0]

    def direct(c, p):
        return all(topo.may_write(c, d) for d in pairs[p])

    def turn(p):
        n = here.index(p)
        return [here[(n + 1) % 3], here[(n + 2) % 3]]

    def order_of(c):
        o = turn(pair_of(c))
        far_off = [not all(direct(d, pair_of(c)) for d in pairs[i]) for i in o]
        return o[::-1] if far_off[1] and not far_off[0] else o

    def blocked(c):
        return [o for o in order_of(c) if not direct(c, o)]

    def helper(c, p):
        can = [h for h in topo.cores_of(c) if h not in T.cores and topo.die(h) == topo.die(c) and direct(h, p)]
        return can[blocked(c).index(p)]

    def on_off(c, other):
        off = topo.engines(c, [d for d in T.cores if topo.host(d) != topo.host(c) and topo.may_write(c, d)][0])
        return off, [e for e in topo.engines(c, other) if e not in off]

    def hop(c, o):
        off, on = on_off(c, helper(c, o))
        if len(blocked(c)) == 1:
            return off + on
        return off if o == blocked(c)[0] else on

    def dst(d):
        rid, pid = topo.addr(d, core)
        return DstId(rid=rid, pnc=pid)

    def peers(c):
        a, b = order_of(c)
        return pairs[a] + pairs[b] + [mate_of(c)]

    def group(c, d):
        return min(peers(c).index(d) // 2, 2)

    sent = [0]

    def fused(transfers):
        ts = []
        for es, src, d, view, s in transfers:
            ts.append(RemoteDMATransfer(dst_ids=[dst(d)], dma_engine_mask=sum(1 << e for e in es), remote_sem=sem[s],
                                        srcs=[src], dsts=[view], alu_op=0))
            sent[0] += len(es)
        g.remote_dma_fused(ts, local_sem=sem.sent)

    def u8(v):
        return v.bitcast(dt.uint8)

    def same(v):
        return v

    def put_list(es, src, c, d):
        j = peers(d).index(c)
        return (es, src[:, local.index(d), :], d, T.ll[:, 8 * j:8 * j + 8], "al%d" % group(d, c))

    rank = T.rank_of(core)
    if rank is None:
        jobs = [(c, o) for c in local for o in turn(pair_of(c)) if not direct(c, o) and helper(c, o) == core]
        if not jobs:
            return
        (c, o), = jobs
        far = topo.engines(core, pairs[o][0])
        h = len(far) // 2
        n = 8 // len(blocked(c))
        j = 8 * peers(c).index(mate_of(c)) + blocked(c).index(o) * n
        g.wait_ge(sem.rlwa, 4)
        fused([(far, T.rlw[:, 0:n], c, T.ll[:, j:j + n], "al2")])
        a = local.index(c) * BK
        for s, buf, lnd, cast in (("rlc", T.rl, T.land, u8), ("rlp", T.rls, T.lands, same)):
            g.wait_ge(sem[s], len(hop(c, o)))
            fused([(far[i * h:i * h + h], cast(buf[:, i * BK:(i + 1) * BK]), d, cast(lnd[:, a:a + BK]), "ap%d" % local.index(c))
                   for i, d in enumerate(pairs[o])])
        g.wait_ge(sem.sent, sent[0])
        return

    p = pair_of(core)
    x = here.index(p)
    away = [o for hh in byhost for o in byhost[hh] if o not in here]
    mate = mate_of(core)
    me = local.index(core)
    order = order_of(core)
    mine = peers(core)
    partner = pairs[away[x]][pairs[p].index(core)]
    far, near = on_off(core, mate)
    h = len(far) // 2
    hb, ab = T.rank_of(local[0]), T.rank_of(pairs[away[0]][0])
    V, S, X = g.vector, g.scalar, g.tensor

    def load(q, buf, src, s, groups):
        for i in groups:
            q.dma_start(buf[16 * i:16 * i + 16], src[:, :]).then_inc(sem[s], 16)

    load(g.sync, T.nd, T.need, "ldn", range(0, 4))
    load(S, T.nd, T.need, "ldn", range(4, 8))
    for i in range(2):
        S.dma_start(T.cin[:, 1024 * i:1024 * i + 1024], T.c[:, 1024 * i:1024 * i + 1024]).then_inc(sem["ldc%d" % i], 16)
    load(g.sync, T.uni32, T.uni, "ldu", range(0, 8))
    g.sync.wait_ge(sem.ldc0, 16)
    g.sync.dma_start(T.win[:, :], T.w[:, :]).then_inc(sem.ldw, 16)
    load(g.sync, T.pos32, T.pos, "ldp", range(0, 8))

    V.wait_ge(sem.ldn, 128)
    V.tensor_scalar(T.lsx[:, :, 0:4], T.nd[:, hb:hb + 6, :], UN, None, AluOpType.add).then_inc(sem.vnd, 1)
    V.tensor_copy(T.lsx[:, :, 4:8], T.nd[:, ab:ab + 6, :]).then_inc(sem.vnd, 1)
    g.wait_ge(sem.vnd, 2)
    if blocked(core):
        fused([(near, T.lsx[:, :, :], mate, T.rli[:, :, :], "al2")])
    straight = [d for o in order if direct(core, o) for d in pairs[o]]
    if straight:
        fused([put_list(far[2 * i:2 * i + 2], T.lsx, core, d) for i, d in enumerate(straight)])
    if blocked(mate):
        n = 8 // len(blocked(mate))
        fused([(near[4 * i:4 * i + 4], T.lsx[:, local.index(mate), n * i:n * i + n], helper(mate, o), T.rlw[:, 0:n], "rlwa")
               for i, o in enumerate(blocked(mate))])
        g.wait_ge(sem.al2, len(near))
        to = [d for o in blocked(mate) for d in pairs[o]]
        n = len(far) // len(to)
        fused([put_list(far[n * i:n * i + n], T.rli, mate, d) for i, d in enumerate(to)])

    def list_count(d):
        if d == mate:
            return len(near) if blocked(d) else len(far) * len(blocked(core))
        return 2 if direct(d, p) else len(far) // (2 * len(blocked(d)))

    for i in range(2):
        a, b = 256 * i, 256 * i + 256
        V.wait_ge(sem["ldc%d" % i], 16)
        V.quantize_mx(T.qc[:, a:b], T.sc[:, a:b], T.cin[:, 4 * a:4 * b]).then_inc(sem.vq, 1)
    V.wait_ge(sem.ldu, 128)
    V.tensor_copy(T.uni16[:, :], T.uni32[:, :]).then_inc(sem.vun, 1)

    def pick(codes, planes, c0, c1, wc, wp, n, off, vs, ss):
        V.tensor_copy(codes[:, c0:c1].bitcast(dt.uint32), wc[:, 0:n].bitcast(dt.uint32).indirect(off)).then_inc(sem[vs], 1)
        S.activation(planes[:, c0:c1], wp[:, 0:n].indirect(off), COPY).then_inc(sem[ss], 1)

    for q in (V, S):
        q.wait_ge(sem.vun, 1)
        q.wait_ge(sem.vq, 2)
    host = topo.host(core)
    o10, h10 = 10 * (1 - host), 10 * host
    pick(T.uo, T.uos, 0, UN, T.qc, T.sc, CT, T.uni16[:, o10:o10 + 10], "vuo", "suo")
    pick(T.uw, T.uws, UN, 2 * UN, T.qc, T.sc, CT, T.uni16[:, h10:h10 + 10], "vuh", "suh")
    g.wait_ge(sem.vuo, 1)
    fused([(far, u8(T.uo[:, :]), partner, u8(T.uw[:, 0:UN]), "auc")])
    g.wait_ge(sem.suo, 1)
    fused([(far, T.uos[:, :], partner, T.uws[:, 0:UN], "aus")])

    V.wait_ge(sem.ldw, 16)
    V.quantize_mx(T.qw[:, :], T.sw[:, :], T.win[:, :]).then_inc(sem.vw, 1)
    own_c, away_c = -BK * hb, CR - BK * ab
    low, high = (own_c, away_c) if hb < ab else (away_c, own_c)
    V.wait_ge(sem.ldp, 128)
    V.tensor_scalar(T.pt[:, :], T.pos32[:, :], -CR, None, AluOpType.bitwise_and).then_inc(sem.vps, 1)
    V.wait_ge(sem.vps, 1)
    V.tensor_tensor(T.pu[:, :], T.pos32[:, :], T.pt[:, :], AluOpType.add).then_inc(sem.vps, 1)
    V.tensor_scalar(T.pv[:, :], T.pt[:, :], 6 * CR, high - low, AluOpType.is_ge, AluOpType.mult).then_inc(sem.vps, 1)
    V.wait_ge(sem.vps, 3)
    V.tensor_tensor(T.pw[:, :], T.pu[:, :], T.pv[:, :], AluOpType.add).then_inc(sem.vps, 1)
    V.wait_ge(sem.vps, 4)
    V.tensor_scalar(T.pos16[:, :], T.pw[:, :], low, None, AluOpType.add).then_inc(sem.vps, 1)

    V.wait_ge(sem.vuh, 1)
    S.wait_ge(sem.suh, 1)
    S.wait_ge(sem.vnd, 2)
    V.wait_ge(sem.vnd, 2)
    V.wait_ge(sem.auc, len(far))
    S.wait_ge(sem.aus, len(far))
    a = me * BK
    for i in range(2):
        for q in (V, S):
            q.wait_ge(sem["al%d" % i], list_count(mine[2 * i]) + list_count(mine[2 * i + 1]))
        pick(T.sd, T.sds, 2 * i * BK, (2 * i + 2) * BK, T.uw, T.uws, 2 * UN, T.ll[:, 16 * i:16 * i + 16], "vsd%d" % i, "ssd%d" % i)
        for vs, buf, lnd, relay, rsem, cast in (("vsd%d" % i, T.sd, T.land, T.rl, "rlc", u8), ("ssd%d" % i, T.sds, T.lands, T.rls, "rlp", same)):
            g.wait_ge(sem[vs], 1)
            if direct(core, order[i]):
                fused([(far[m * h:m * h + h], cast(buf[:, (2 * i + m) * BK:(2 * i + m + 1) * BK]), d, cast(lnd[:, a:a + BK]), "ap%d" % me)
                       for m, d in enumerate(pairs[order[i]])])
            else:
                fused([(hop(core, order[i]), cast(buf[:, 2 * i * BK:(2 * i + 2) * BK]), helper(core, order[i]), cast(relay[:, :]), rsem)])
    pick(T.land, T.lands, a, a + BK, T.uw, T.uws, 2 * UN, T.lsx[:, me, :], "vown", "sown")
    for q in (V, S):
        q.wait_ge(sem.al2, list_count(mate))
    off = T.rli[:, me, :] if blocked(mate) else T.ll[:, 32:40]
    pick(T.sd, T.sds, 4 * BK, 5 * BK, T.uw, T.uws, 2 * UN, off, "vsd2", "ssd2")
    for vs, buf, lnd, cast in (("vsd2", T.sd, T.land, u8), ("ssd2", T.sds, T.lands, same)):
        g.wait_ge(sem[vs], 1)
        fused([(near, cast(buf[:, 4 * BK:5 * BK]), mate, cast(lnd[:, a:a + BK]), "ap%d" % me)])

    seq = [core, mate] + [d for d in mine[:4] if direct(d, p)] + [d for d in mine[:4] if not direct(d, p)]
    X.wait_ge(sem.vw, 1)
    for i, d in enumerate(seq):
        j = local.index(d)
        if d == core:
            X.wait_ge(sem.vown, 1)
            X.wait_ge(sem.sown, 1)
        else:
            X.wait_ge(sem["ap%d" % j], 2 * len(near) if d == mate else 2 * h)
        b = j * BK
        X.matmul_mx(T.acc[:, 512 * i:512 * i + BK], T.qw[:, :], T.sw[:, :], T.land[:, b:b + BK], T.lands[:, b:b + BK], True, True).then_inc(sem["tm%d" % i], 1)
        q = (S, V)[i % 2]
        q.wait_ge(sem["tm%d" % i], 1)
        if i % 2:
            V.tensor_copy(T.ys[:, b:b + BK], T.acc[:, 512 * i:512 * i + BK]).then_inc(sem.evv, 1)
        else:
            S.activation(T.ys[:, b:b + BK], T.acc[:, 512 * i:512 * i + BK], COPY).then_inc(sem.evs, 1)

    for q in (V, S):
        q.wait_ge(sem.evv, 3)
        q.wait_ge(sem.evs, 3)
        q.wait_ge(sem.vps, 5)
    V.tensor_copy(T.yo[:, 0:256], T.ys[:, :].indirect(T.pos16[:, 0:16])).then_inc(sem.gv, 1)
    S.activation(T.yo[:, 256:512], T.ys[:, :].indirect(T.pos16[:, 16:32]), COPY).then_inc(sem.gs, 1)
    g.sync.wait_ge(sem.gv, 1)
    g.sync.wait_ge(sem.gs, 1)
    g.sync.dma_start(T.y[:, :], T.yo[:, :]).then_inc(sem.st0, 16)
    g.sync.wait_ge(sem.st0, 16)
    g.wait_ge(sem.sent, sent[0])
